import numpy as np
import ml_dtypes

BF16 = ml_dtypes.bfloat16


def bf(x):
    return np.asarray(x, np.float32).astype(BF16)


def f32(x):
    return np.asarray(x, np.float32)


def f64(x):
    return np.asarray(x).astype(np.float64)


def striped(idx):
    return np.tile(idx.reshape(-1, 16).T, (8, 1))


S, K, M, N, E, Q = 256, 256, 256, 256, 2, 128


def setup_inputs():
    return {"base": bf(np.random.standard_normal((M, S))), "x": bf(np.random.standard_normal((K, N))), "w": bf(np.random.standard_normal((E, K, M)) / np.sqrt(K)), "b": f32(0.5 * np.random.standard_normal((M, 1))), "offs": striped(np.random.permutation(S))}


def reference(base, x, w, b, offs):
    idx = offs[:16].T.reshape(-1)
    z = f64(base).copy()
    for e in range(E):
        z[:, idx[e * Q : (e + 1) * Q]] += f64(w)[e].T @ f64(x)[:, e * Q : (e + 1) * Q]
    return np.tanh(z + f64(b))

@@ -1,0 +1,64 @@
+import concourse.mybir as mybir
+from concourse.masks import make_identity
+
+P = 128
+S = 256
+K = 256
+M = 256
+E = 2
+Q = 128
+KB = K // P
+MB = M // P
+OFFSETS_PER_COLUMN = 16
+
+FLOPS = 2 * K * M * E * Q
+
+BF16 = mybir.dt.bfloat16
+F32 = mybir.dt.float32
+U16 = mybir.dt.uint16
+TANH = mybir.ActivationFunctionType.Tanh
+
+
+def tile_scatter_matmul_kernel(tc, base, x, w, b, offs, out):
+    nc = tc.nc
+    with (
+        tc.tile_pool(name="held", bufs=1) as held,
+        tc.psum_pool(name="windows", bufs=1) as windows,
+    ):
+        offsets = held.tile([P, E * Q // OFFSETS_PER_COLUMN], U16, name="offsets")
+        nc.sync.dma_start(offsets[:], offs)
+
+        base_sb = held.tile([P, MB, S], BF16, name="base_sb")
+        nc.sync.dma_start(base_sb[:], base.rearrange("(a p) s -> p a s", p=P))
+        x_sb = held.tile([P, KB, E * Q], BF16, name="x_sb")
+        nc.sync.dma_start(x_sb[:], x.rearrange("(a p) j -> p a j", p=P))
+        w_sb = [held.tile([P, KB, M], BF16, name="w_sb%d" % e) for e in range(E)]
+        for e in range(E):
+            nc.scalar.dma_start(w_sb[e][:], w[e].rearrange("(a p) m -> p a m", p=P))
+
+        bias_sb = held.tile([P, MB], F32, name="bias_sb")
+        with nc.allow_non_contiguous_dma(reason="one 4-byte bias value to a partition"):
+            nc.scalar.dma_start(bias_sb[:], b.rearrange("(a p) o -> p (a o)", p=P))
+
+        identity = held.tile([P, P], BF16, name="identity")
+        make_identity(nc, identity[:])
+
+        window = [windows.tile([P, S], F32, name="window%d" % mb) for mb in range(MB)]
+        for mb in range(MB):
+            nc.tensor.matmul(window[mb][:], identity[:], base_sb[:, mb, :], start=True, stop=False)
+
+        out_sb = held.tile([P, MB, S], F32, name="out_sb")
+        for mb in range(MB):
+            for e in range(E):
+                piece = offsets[:, e * Q // OFFSETS_PER_COLUMN : (e + 1) * Q // OFFSETS_PER_COLUMN]
+                for kb in range(KB):
+                    last = e == E - 1 and kb == KB - 1
+                    nc.tensor.matmul(
+                        window[mb][:].indirect(piece),
+                        w_sb[e][:, kb, mb * P : (mb + 1) * P],
+                        x_sb[:, kb, e * Q : (e + 1) * Q],
+                        start=False,
+                        stop=last,
+                    )
+            nc.scalar.activation(out_sb[:, mb, :], window[mb][:], TANH, bias=bias_sb[:, mb : mb + 1])
+            nc.sync.dma_start(out[mb * P : (mb + 1) * P, :], out_sb[:, mb, :])

@@ -10,6 +10,7 @@ Q = 128
 KB = K // P
 MB = M // P
 OFFSETS_PER_COLUMN = 16
+WARM_MATMULS = 12
 
 FLOPS = 2 * K * M * E * Q
 
@@ -29,16 +30,23 @@ def tile_scatter_matmul_kernel(tc, base, x, w, b, offs, out):
         nc.sync.dma_start(offsets[:], offs)
 
         base_sb = held.tile([P, MB, S], BF16, name="base_sb")
-        nc.sync.dma_start(base_sb[:], base.rearrange("(a p) s -> p a s", p=P))
+        nc.scalar.dma_start(base_sb[:], base.rearrange("(a p) s -> p a s", p=P))
         x_sb = held.tile([P, KB, E * Q], BF16, name="x_sb")
         nc.sync.dma_start(x_sb[:], x.rearrange("(a p) j -> p a j", p=P))
         w_sb = [held.tile([P, KB, M], BF16, name="w_sb%d" % e) for e in range(E)]
-        for e in range(E):
-            nc.scalar.dma_start(w_sb[e][:], w[e].rearrange("(a p) m -> p a m", p=P))
-
+        nc.scalar.dma_start(w_sb[0][:], w[0].rearrange("(a p) m -> p a m", p=P))
+        nc.sync.dma_start(w_sb[1][:], w[1].rearrange("(a p) m -> p a m", p=P))
         bias_sb = held.tile([P, MB], F32, name="bias_sb")
         with nc.allow_non_contiguous_dma(reason="one 4-byte bias value to a partition"):
             nc.scalar.dma_start(bias_sb[:], b.rearrange("(a p) o -> p (a o)", p=P))
+
+        zeros = held.tile([P, P], BF16, name="zeros")
+        nc.gpsimd.memset(zeros[:], 0.0)
+        warm = windows.tile([P, P], F32, name="warm")
+        for i in range(WARM_MATMULS):
+            nc.tensor.matmul(warm[:], zeros[:], zeros[:], start=True, stop=True)
+        early_tanh = held.tile([P, 1], F32, name="early_tanh")
+        nc.scalar.activation(early_tanh[:], zeros[:, 0:1], TANH)
 
         identity = held.tile([P, P], BF16, name="identity")
         make_identity(nc, identity[:])
@@ -47,10 +55,9 @@ def tile_scatter_matmul_kernel(tc, base, x, w, b, offs, out):
         for mb in range(MB):
             nc.tensor.matmul(window[mb][:], identity[:], base_sb[:, mb, :], start=True, stop=False)
 
-        out_sb = held.tile([P, MB, S], F32, name="out_sb")
-        for mb in range(MB):
-            for e in range(E):
-                piece = offsets[:, e * Q // OFFSETS_PER_COLUMN : (e + 1) * Q // OFFSETS_PER_COLUMN]
+        for e in range(E):
+            piece = offsets[:, e * Q // OFFSETS_PER_COLUMN : (e + 1) * Q // OFFSETS_PER_COLUMN]
+            for mb in range(MB):
                 for kb in range(KB):
                     last = e == E - 1 and kb == KB - 1
                     nc.tensor.matmul(
@@ -60,5 +67,8 @@ def tile_scatter_matmul_kernel(tc, base, x, w, b, offs, out):
                         start=False,
                         stop=last,
                     )
+
+        out_sb = held.tile([P, MB, S], F32, name="out_sb")
+        for mb in range(MB):
             nc.scalar.activation(out_sb[:, mb, :], window[mb][:], TANH, bias=bias_sb[:, mb : mb + 1])
             nc.sync.dma_start(out[mb * P : (mb + 1) * P, :], out_sb[:, mb, :])

@@ -30,15 +30,15 @@ def tile_scatter_matmul_kernel(tc, base, x, w, b, offs, out):
         nc.sync.dma_start(offsets[:], offs)
 
         base_sb = held.tile([P, MB, S], BF16, name="base_sb")
-        nc.scalar.dma_start(base_sb[:], base.rearrange("(a p) s -> p a s", p=P))
+        nc.sync.dma_start(base_sb[:], base.rearrange("(a p) s -> p a s", p=P))
         x_sb = held.tile([P, KB, E * Q], BF16, name="x_sb")
         nc.sync.dma_start(x_sb[:], x.rearrange("(a p) j -> p a j", p=P))
         w_sb = [held.tile([P, KB, M], BF16, name="w_sb%d" % e) for e in range(E)]
-        nc.scalar.dma_start(w_sb[0][:], w[0].rearrange("(a p) m -> p a m", p=P))
+        nc.sync.dma_start(w_sb[0][:], w[0].rearrange("(a p) m -> p a m", p=P))
         nc.sync.dma_start(w_sb[1][:], w[1].rearrange("(a p) m -> p a m", p=P))
         bias_sb = held.tile([P, MB], F32, name="bias_sb")
         with nc.allow_non_contiguous_dma(reason="one 4-byte bias value to a partition"):
-            nc.scalar.dma_start(bias_sb[:], b.rearrange("(a p) o -> p (a o)", p=P))
+            nc.sync.dma_start(bias_sb[:], b.rearrange("(a p) o -> p (a o)", p=P))
 
         zeros = held.tile([P, P], BF16, name="zeros")
         nc.gpsimd.memset(zeros[:], 0.0)

@@ -32,10 +32,10 @@ def tile_scatter_matmul_kernel(tc, base, x, w, b, offs, out):
         base_sb = held.tile([P, MB, S], BF16, name="base_sb")
         nc.sync.dma_start(base_sb[:], base.rearrange("(a p) s -> p a s", p=P))
         x_sb = held.tile([P, KB, E * Q], BF16, name="x_sb")
-        nc.sync.dma_start(x_sb[:], x.rearrange("(a p) j -> p a j", p=P))
+        nc.sync.dma_start(x_sb[:], x.rearrange("(p a) j -> p a j", a=KB))
         w_sb = [held.tile([P, KB, M], BF16, name="w_sb%d" % e) for e in range(E)]
-        nc.sync.dma_start(w_sb[0][:], w[0].rearrange("(a p) m -> p a m", p=P))
-        nc.sync.dma_start(w_sb[1][:], w[1].rearrange("(a p) m -> p a m", p=P))
+        nc.sync.dma_start(w_sb[0][:], w[0].rearrange("(p a) m -> p a m", a=KB))
+        nc.sync.dma_start(w_sb[1][:], w[1].rearrange("(p a) m -> p a m", a=KB))
         bias_sb = held.tile([P, MB], F32, name="bias_sb")
         with nc.allow_non_contiguous_dma(reason="one 4-byte bias value to a partition"):
             nc.sync.dma_start(bias_sb[:], b.rearrange("(a p) o -> p (a o)", p=P))

@@ -26,11 +26,10 @@ def tile_scatter_matmul_kernel(tc, base, x, w, b, offs, out):
         tc.tile_pool(name="held", bufs=1) as held,
         tc.psum_pool(name="windows", bufs=1) as windows,
     ):
-        offsets = held.tile([P, E * Q // OFFSETS_PER_COLUMN], U16, name="offsets")
-        nc.sync.dma_start(offsets[:], offs)
-
         base_sb = held.tile([P, MB, S], BF16, name="base_sb")
         nc.sync.dma_start(base_sb[:], base.rearrange("(a p) s -> p a s", p=P))
+        offsets = held.tile([P, E * Q // OFFSETS_PER_COLUMN], U16, name="offsets")
+        nc.sync.dma_start(offsets[:], offs)
         x_sb = held.tile([P, KB, E * Q], BF16, name="x_sb")
         nc.sync.dma_start(x_sb[:], x.rearrange("(p a) j -> p a j", a=KB))
         w_sb = [held.tile([P, KB, M], BF16, name="w_sb%d" % e) for e in range(E)]

@@ -10,6 +10,7 @@ Q = 128
 KB = K // P
 MB = M // P
 OFFSETS_PER_COLUMN = 16
+ROW_ALIGN = 256
 WARM_MATMULS = 12
 
 FLOPS = 2 * K * M * E * Q
@@ -26,13 +27,13 @@ def tile_scatter_matmul_kernel(tc, base, x, w, b, offs, out):
         tc.tile_pool(name="held", bufs=1) as held,
         tc.psum_pool(name="windows", bufs=1) as windows,
     ):
-        base_sb = held.tile([P, MB, S], BF16, name="base_sb")
+        base_sb = held.tile([P, MB, S], BF16, name="base_sb", align_bytes=ROW_ALIGN)
         nc.sync.dma_start(base_sb[:], base.rearrange("(a p) s -> p a s", p=P))
         offsets = held.tile([P, E * Q // OFFSETS_PER_COLUMN], U16, name="offsets")
         nc.sync.dma_start(offsets[:], offs)
-        x_sb = held.tile([P, KB, E * Q], BF16, name="x_sb")
+        x_sb = held.tile([P, KB, E * Q], BF16, name="x_sb", align_bytes=ROW_ALIGN)
         nc.sync.dma_start(x_sb[:], x.rearrange("(p a) j -> p a j", a=KB))
-        w_sb = [held.tile([P, KB, M], BF16, name="w_sb%d" % e) for e in range(E)]
+        w_sb = [held.tile([P, KB, M], BF16, name="w_sb%d" % e, align_bytes=ROW_ALIGN) for e in range(E)]
         nc.sync.dma_start(w_sb[0][:], w[0].rearrange("(p a) m -> p a m", a=KB))
         nc.sync.dma_start(w_sb[1][:], w[1].rearrange("(p a) m -> p a m", a=KB))
         bias_sb = held.tile([P, MB], F32, name="bias_sb")
@@ -67,7 +68,7 @@ def tile_scatter_matmul_kernel(tc, base, x, w, b, offs, out):
                         stop=last,
                     )
 
-        out_sb = held.tile([P, MB, S], F32, name="out_sb")
+        out_sb = held.tile([P, MB, S], F32, name="out_sb", align_bytes=ROW_ALIGN)
         for mb in range(MB):
             nc.scalar.activation(out_sb[:, mb, :], window[mb][:], TANH, bias=bias_sb[:, mb : mb + 1])
             nc.sync.dma_start(out[mb * P : (mb + 1) * P, :], out_sb[:, mb, :])

@@ -11,7 +11,7 @@ KB = K // P
 MB = M // P
 OFFSETS_PER_COLUMN = 16
 ROW_ALIGN = 256
-WARM_MATMULS = 12
+WARM_MATMULS = 8
 
 FLOPS = 2 * K * M * E * Q
 

@@ -40,11 +40,12 @@ def tile_scatter_matmul_kernel(tc, base, x, w, b, offs, out):
         with nc.allow_non_contiguous_dma(reason="one 4-byte bias value to a partition"):
             nc.sync.dma_start(bias_sb[:], b.rearrange("(a p) o -> p (a o)", p=P))
 
-        zeros = held.tile([P, P], BF16, name="zeros")
+        zeros = held.tile([P, 2], BF16, name="zeros")
         nc.gpsimd.memset(zeros[:], 0.0)
+        zero_block = zeros[:, 0:1].to_broadcast([P, P])
         warm = windows.tile([P, P], F32, name="warm")
         for i in range(WARM_MATMULS):
-            nc.tensor.matmul(warm[:], zeros[:], zeros[:], start=True, stop=True)
+            nc.tensor.matmul(warm[:], zero_block, zero_block, start=True, stop=True)
         early_tanh = held.tile([P, 1], F32, name="early_tanh")
         nc.scalar.activation(early_tanh[:], zeros[:, 0:1], TANH)
 

@@ -56,18 +56,17 @@ def tile_scatter_matmul_kernel(tc, base, x, w, b, offs, out):
         for mb in range(MB):
             nc.tensor.matmul(window[mb][:], identity[:], base_sb[:, mb, :], start=True, stop=False)
 
-        for e in range(E):
-            piece = offsets[:, e * Q // OFFSETS_PER_COLUMN : (e + 1) * Q // OFFSETS_PER_COLUMN]
-            for mb in range(MB):
-                for kb in range(KB):
-                    last = e == E - 1 and kb == KB - 1
-                    nc.tensor.matmul(
-                        window[mb][:].indirect(piece),
-                        w_sb[e][:, kb, mb * P : (mb + 1) * P],
-                        x_sb[:, kb, e * Q : (e + 1) * Q],
-                        start=False,
-                        stop=last,
-                    )
+        expert0 = [(0, mb, kb) for kb in range(KB) for mb in range(MB)]
+        into_window0 = [(1, 0, kb) for kb in range(KB)]
+        into_window1 = [(1, 1, kb) for kb in range(KB)]
+        for e, mb, kb in expert0[:-1] + into_window0 + expert0[-1:] + into_window1:
+            nc.tensor.matmul(
+                window[mb][:].indirect(offsets[:, e * Q // OFFSETS_PER_COLUMN : (e + 1) * Q // OFFSETS_PER_COLUMN]),
+                w_sb[e][:, kb, mb * P : (mb + 1) * P],
+                x_sb[:, kb, e * Q : (e + 1) * Q],
+                start=False,
+                stop=e == E - 1 and kb == KB - 1,
+            )
 
         out_sb = held.tile([P, MB, S], F32, name="out_sb", align_bytes=ROW_ALIGN)
         for mb in range(MB):

@@ -1,5 +1,4 @@
 import concourse.mybir as mybir
-from concourse.masks import make_identity
 
 P = 128
 S = 256
@@ -28,7 +27,7 @@ def tile_scatter_matmul_kernel(tc, base, x, w, b, offs, out):
         tc.psum_pool(name="windows", bufs=1) as windows,
     ):
         base_sb = held.tile([P, MB, S], BF16, name="base_sb", align_bytes=ROW_ALIGN)
-        nc.sync.dma_start(base_sb[:], base.rearrange("(a p) s -> p a s", p=P))
+        nc.sync.dma_start(base_sb[:], base.rearrange("(p a) s -> p a s", a=MB))
         offsets = held.tile([P, E * Q // OFFSETS_PER_COLUMN], U16, name="offsets")
         nc.sync.dma_start(offsets[:], offs)
         x_sb = held.tile([P, KB, E * Q], BF16, name="x_sb", align_bytes=ROW_ALIGN)
@@ -49,12 +48,23 @@ def tile_scatter_matmul_kernel(tc, base, x, w, b, offs, out):
         early_tanh = held.tile([P, 1], F32, name="early_tanh")
         nc.scalar.activation(early_tanh[:], zeros[:, 0:1], TANH)
 
-        identity = held.tile([P, P], BF16, name="identity")
-        make_identity(nc, identity[:])
+        even = held.tile([P, 2 + M], BF16, name="even")
+        nc.gpsimd.memset(even[:], 0.0)
+        nc.gpsimd.affine_select(
+            out=even[:],
+            in_=even[:],
+            compare_op=mybir.AluOpType.not_equal,
+            fill=1.0,
+            base=1,
+            pattern=[[-1, 2 + M]],
+            channel_multiplier=2,
+        )
 
         window = [windows.tile([P, S], F32, name="window%d" % mb) for mb in range(MB)]
         for mb in range(MB):
-            nc.tensor.matmul(window[mb][:], identity[:], base_sb[:, mb, :], start=True, stop=False)
+            for a in range(MB):
+                pick = even[:, 1 - a + mb * P : 1 - a + (mb + 1) * P]
+                nc.tensor.matmul(window[mb][:], pick, base_sb[:, a, :], start=a == 0, stop=False)
 
         expert0 = [(0, mb, kb) for kb in range(KB) for mb in range(MB)]
         into_window0 = [(1, 0, kb) for kb in range(KB)]

import concourse.mybir as mybir

P = 128
S = 256
K = 256
M = 256
E = 2
Q = 128
KB = K // P
MB = M // P
OFFSETS_PER_COLUMN = 16
ROW_ALIGN = 256
WARM_MATMULS = 8

FLOPS = 2 * K * M * E * Q

BF16 = mybir.dt.bfloat16
F32 = mybir.dt.float32
U16 = mybir.dt.uint16
TANH = mybir.ActivationFunctionType.Tanh


def tile_scatter_matmul_kernel(tc, base, x, w, b, offs, out):
    nc = tc.nc
    with (
        tc.tile_pool(name="held", bufs=1) as held,
        tc.psum_pool(name="windows", bufs=1) as windows,
    ):
        base_sb = held.tile([P, MB, S], BF16, name="base_sb", align_bytes=ROW_ALIGN)
        nc.sync.dma_start(base_sb[:], base.rearrange("(p a) s -> p a s", a=MB))
        offsets = held.tile([P, E * Q // OFFSETS_PER_COLUMN], U16, name="offsets")
        nc.sync.dma_start(offsets[:], offs)
        x_sb = held.tile([P, KB, E * Q], BF16, name="x_sb", align_bytes=ROW_ALIGN)
        nc.sync.dma_start(x_sb[:], x.rearrange("(p a) j -> p a j", a=KB))
        w_sb = [held.tile([P, KB, M], BF16, name="w_sb%d" % e, align_bytes=ROW_ALIGN) for e in range(E)]
        nc.sync.dma_start(w_sb[0][:], w[0].rearrange("(p a) m -> p a m", a=KB))
        nc.sync.dma_start(w_sb[1][:], w[1].rearrange("(p a) m -> p a m", a=KB))
        bias_sb = held.tile([P, MB], F32, name="bias_sb")
        with nc.allow_non_contiguous_dma(reason="one 4-byte bias value to a partition"):
            nc.sync.dma_start(bias_sb[:], b.rearrange("(a p) o -> p (a o)", p=P))

        zeros = held.tile([P, 2], BF16, name="zeros")
        nc.gpsimd.memset(zeros[:], 0.0)
        zero_block = zeros[:, 0:1].to_broadcast([P, P])
        warm = windows.tile([P, P], F32, name="warm")
        for i in range(WARM_MATMULS):
            nc.tensor.matmul(warm[:], zero_block, zero_block, start=True, stop=True)
        early_tanh = held.tile([P, 1], F32, name="early_tanh")
        nc.scalar.activation(early_tanh[:], zeros[:, 0:1], TANH)

        even = held.tile([P, 2 + M], BF16, name="even")
        nc.gpsimd.memset(even[:], 0.0)
        nc.gpsimd.affine_select(
            out=even[:],
            in_=even[:],
            compare_op=mybir.AluOpType.not_equal,
            fill=1.0,
            base=1,
            pattern=[[-1, 2 + M]],
            channel_multiplier=2,
        )

        window = [windows.tile([P, S], F32, name="window%d" % mb) for mb in range(MB)]
        for mb in range(MB):
            for a in range(MB):
                pick = even[:, 1 - a + mb * P : 1 - a + (mb + 1) * P]
                nc.tensor.matmul(window[mb][:], pick, base_sb[:, a, :], start=a == 0, stop=False)

        expert0 = [(0, mb, kb) for kb in range(KB) for mb in range(MB)]
        into_window0 = [(1, 0, kb) for kb in range(KB)]
        into_window1 = [(1, 1, kb) for kb in range(KB)]
        for e, mb, kb in expert0[:-1] + into_window0 + expert0[-1:] + into_window1:
            nc.tensor.matmul(
                window[mb][:].indirect(offsets[:, e * Q // OFFSETS_PER_COLUMN : (e + 1) * Q // OFFSETS_PER_COLUMN]),
                w_sb[e][:, kb, mb * P : (mb + 1) * P],
                x_sb[:, kb, e * Q : (e + 1) * Q],
                start=False,
                stop=e == E - 1 and kb == KB - 1,
            )

        out_sb = held.tile([P, MB, S], F32, name="out_sb", align_bytes=ROW_ALIGN)
        for mb in range(MB):
            nc.scalar.activation(out_sb[:, mb, :], window[mb][:], TANH, bias=bias_sb[:, mb : mb + 1])
            nc.sync.dma_start(out[mb * P : (mb + 1) * P, :], out_sb[:, mb, :])
